import numpy as np
import ml_dtypes


def mxq(x, axis, fmt="e4m3"):
    dtype, down = {"e4m3": (ml_dtypes.float8_e4m3fn, 7), "e5m2": (ml_dtypes.float8_e5m2, 14)}[fmt]
    v = np.moveaxis(np.asarray(x, np.float32).astype(ml_dtypes.bfloat16).astype(np.float64), axis, -1)
    blocks = v.reshape(v.shape[:-1] + (-1, 32))
    amax = np.abs(blocks).max(-1, keepdims=True)
    byte = np.maximum(np.where(amax > 0, np.frexp(amax)[1] - 1 + 127, 0) - down, 1)
    scale = np.exp2(byte - 127.0)
    codes = (blocks / scale).astype(np.float32).astype(dtype).astype(np.float64)
    return np.moveaxis((codes * scale).reshape(v.shape), -1, axis)


WIDE = False


def mx_kscale(k):
    if not WIDE:
        return np.ones(k)
    levels = np.array([10, -10, 5, -5, 0])
    if k % 512:
        return np.exp2(np.random.permutation(np.resize(levels, k // 32))).repeat(32)
    a = np.empty((k // 512, 16))
    for p in range(k // 512):
        a[p, :8] = np.random.permutation(np.resize(levels, 8))
        for g in range(8):
            far = levels[np.abs(levels - a[p, g]) >= 10]
            a[p, g + 8] = far[np.random.randint(len(far))]
    return np.exp2(a.ravel()).repeat(32)


def f64(x):
    return np.asarray(x).astype(np.float64)


def striped(idx):
    return np.tile(idx.reshape(-1, 16).T, (8, 1)).astype(np.uint16)


def unstriped(offs):
    return offs[:16].T.reshape(-1).astype(np.int64)


def pack_weight(w):
    k, n = w.shape
    w = f64(np.asarray(w, np.float32).astype(ml_dtypes.bfloat16)).reshape(k // 32, 32, n)
    amax = np.abs(w).max(1)
    byte = np.clip(np.where(amax > 0, np.frexp(amax)[1] - 1 + 127 - 7, 1), 1, 254)
    scaled = (w * np.exp2(127.0 - byte)[:, None, :]).reshape(k, n).astype(np.float32)
    words = np.ascontiguousarray(scaled.reshape(k // 512, 128, 4, n).transpose(0, 1, 3, 2)).astype(ml_dtypes.float8_e4m3fn).view(np.uint8)
    return words, np.ascontiguousarray(byte.astype(np.uint8).reshape(k // 512, 16, n))


def unpack_weight(words, scales):
    g, p, n, _ = words.shape
    vals = np.ascontiguousarray(words).view(ml_dtypes.float8_e4m3fn).astype(np.float64) * np.repeat(np.exp2(scales.astype(np.float64) - 127.0), 8, axis=1)[..., None]
    return vals.transpose(0, 1, 3, 2).reshape(g * 512, n)


def relu(v):
    return np.maximum(v, 0.0)


def sigmoid(v):
    return 1.0 / (1.0 + np.exp(-np.maximum(v, -700.0)))


K, T, N = 1024, 1024, 128


def setup_inputs():
    n = np.random.standard_normal
    s = mx_kscale(K)[:, None]
    packed_xT = pack_weight(n((K, T)) * s)
    return {
        "x_words": packed_xT[0],
        "x_scales": packed_xT[1],
        "w1": (n((K, N)) / np.sqrt(K) / s).astype(np.float32),
        "w2": (n((K, N)) / np.sqrt(K) / s).astype(np.float32),
        "w3": (n((K, N)) / np.sqrt(K) / s).astype(np.float32),
        "pos1": striped(np.random.permutation(T)),
        "pos2": striped(np.random.permutation(T)),
    }


def reference(x_words, x_scales, w1, w2, w3, pos1, pos2):
    xq = unpack_weight(x_words, x_scales)
    y = mxq(f64(w1), 0, "e4m3").T @ xq
    e = mxq(f64(w2), 0, "e4m3").T @ xq
    h = mxq(f64(w3), 0, "e4m3").T @ xq
    z = (sigmoid(y + e[:, unstriped(pos1)])) * h[:, unstriped(pos1)] + (sigmoid(y + e[:, unstriped(pos2)])) * h[:, unstriped(pos2)]
    return relu(z)

@@ -1,0 +1,159 @@
+from contextlib import ExitStack
+
+import concourse.mybir as mybir
+
+K, T, M = 1024, 1024, 128
+FLOPS = 3 * 2 * K * T * M
+
+F32 = mybir.dt.float32
+BF16 = mybir.dt.bfloat16
+I32 = mybir.dt.int32
+U32 = mybir.dt.uint32
+U16 = mybir.dt.uint16
+U8 = mybir.dt.uint8
+FP8X4 = mybir.dt.float8_e4m3fn_x4
+ALU = mybir.AluOpType
+ACT = mybir.ActivationFunctionType
+
+P = 128
+PACK = 4
+K_PASS = P * PACK
+PASSES = K // K_PASS
+BANK = 512
+HALVES = T // BANK
+LANES = 16
+OUT_CHUNKS = ((0, 512), (512, 768), (768, 896), (896, 1024))
+
+
+def tile_picked_wgatedg_relu_l_kernel(
+    tc, x_words, x_scales, w1, w2, w3, pos1, pos2, out
+):
+    nc = tc.nc
+
+    def interleave(copy, grouped, raw):
+        copy(
+            grouped.rearrange("p (c i t) -> p c t i", i=4, t=PACK),
+            raw.rearrange("p (t c i) -> p c t i", i=4, t=PACK),
+        )
+
+    def weight_rows(w):
+        return w.rearrange("(z p t) m -> p z (t m)", z=PASSES, t=PACK)
+
+    with ExitStack() as ctx:
+        keep = ctx.enter_context(tc.tile_pool(name="keep", bufs=1))
+        psum = ctx.enter_context(tc.psum_pool(name="psum", bufs=1))
+
+        lists = [keep.tile([P, T // LANES], U16, name=f"list{d}") for d in range(2)]
+        x_plane = keep.tile([P, T], U8, align_bytes=64)
+        nc.vector.memset(x_plane[:].bitcast(I32), 0)
+
+        w2_raw = [keep.tile([P, K_PASS], F32, name=f"w2_raw{z}") for z in range(PASSES)]
+        for z in range(PASSES):
+            nc.sync.dma_start(w2_raw[z][:], weight_rows(w2)[:, z, :])
+        for q in range(4):
+            nc.scalar.dma_start(
+                x_plane[32 * q : 32 * q + 4 * PASSES, :].bitcast(I32),
+                x_scales[:, 4 * q : 4 * q + 4, :].bitcast(I32),
+            )
+
+        x_codes = {}
+        for c in range(HALVES):
+            for z in range(PASSES):
+                x_codes[z, c] = keep.tile([P, BANK], U32, name=f"x_codes{z}{c}", align_bytes=64)
+                words = x_words[z].rearrange("p n t -> p (n t)")
+                nc.sync.dma_start(
+                    x_codes[z, c][:].bitcast(I32),
+                    words[:, PACK * BANK * c : PACK * BANK * (c + 1)].bitcast(I32),
+                )
+        nc.sync.dma_start(lists[0][:], pos1)
+        w1_raw = keep.tile([P, PASSES, K_PASS], F32)
+        nc.sync.dma_start(w1_raw[:], weight_rows(w1))
+        nc.sync.dma_start(lists[1][:], pos2)
+        w3_raw = keep.tile([P, PASSES, K_PASS], F32)
+        nc.sync.dma_start(w3_raw[:], weight_rows(w3))
+
+        def product(acc, codes, plane, c, lo, hi):
+            for z in range(PASSES):
+                nc.tensor.matmul_mx(
+                    acc,
+                    lhsT=codes[z].bitcast(FP8X4),
+                    lhsT_scale=plane[z],
+                    rhs=x_codes[z, c][:, lo:hi].bitcast(FP8X4),
+                    rhs_scale=x_plane[4 * z : P, BANK * c + lo : BANK * c + hi],
+                    start=(z == 0),
+                    stop=(z == PASSES - 1),
+                )
+
+        w2_codes, w2_plane = [], []
+        for z in range(PASSES):
+            grouped = keep.tile([P, K_PASS], BF16, name=f"w2_grouped{z}", align_bytes=64)
+            codes = keep.tile([P, M], U32, name=f"w2_codes{z}", align_bytes=64)
+            plane = keep.tile([P, M], U8, name=f"w2_plane{z}", align_bytes=64)
+            interleave(nc.vector.tensor_copy, grouped[:], w2_raw[z][:])
+            nc.vector.quantize_mx(codes[:].bitcast(FP8X4), plane[:], grouped[:])
+            w2_codes.append(codes[:])
+            w2_plane.append(plane[:])
+        e = keep.tile([P, T], F32)
+        e_pieces = ((0, 0, 512, nc.scalar.copy), (1, 0, 256, nc.scalar.copy), (1, 256, 512, nc.vector.tensor_copy))
+        for i, (c, lo, hi, copy) in enumerate(e_pieces):
+            acc = psum.tile([P, hi - lo], F32, name=f"e_acc{i}")
+            product(acc[:], w2_codes, w2_plane, c, lo, hi)
+            copy(e[:, BANK * c + lo : BANK * c + hi], acc[:])
+
+        def offsets(d, lo, hi):
+            return lists[d][:, lo // LANES : hi // LANES]
+
+        def quantized(raw, tag):
+            grouped = keep.tile([P, K], BF16, name=tag + "_grouped", tag=tag, align_bytes=64)
+            codes = keep.tile([P, PASSES * M], U32, name=tag + "_codes", align_bytes=64)
+            plane = keep.tile([P, PASSES * M], U8, name=tag + "_plane", align_bytes=64)
+            for z in range(PASSES):
+                interleave(nc.scalar.copy, grouped[:, K_PASS * z : K_PASS * (z + 1)], raw[:, z, :])
+            nc.vector.quantize_mx(codes[:].bitcast(FP8X4), plane[:], grouped[:])
+            return (
+                [codes[:, M * z : M * (z + 1)] for z in range(PASSES)],
+                [plane[:, M * z : M * (z + 1)] for z in range(PASSES)],
+            )
+
+        e_picked = {}
+
+        def pick_e(d, c, tag):
+            e_picked[d, c] = keep.tile([P, BANK], F32, name=f"e_picked{d}{c}", tag=tag, align_bytes=64)
+            nc.vector.tensor_copy(e_picked[d, c][:], e[:].indirect(offsets(d, BANK * c, BANK * (c + 1))))
+
+        pick_e(0, 0, "pick00")
+        pick_e(1, 0, "pick10")
+        w1_codes, w1_plane = quantized(w1_raw, "w1")
+        y_acc = []
+        for c in range(HALVES):
+            acc = psum.tile([P, BANK], F32, name=f"y_acc{c}")
+            product(acc[:], w1_codes, w1_plane, c, 0, BANK)
+            y_acc.append(acc)
+        pick_e(0, 1, "w1")
+        w3_codes, w3_plane = quantized(w3_raw, "w3")
+        h = keep.tile([P, T], F32)
+        h_acc = []
+        for c in range(HALVES):
+            acc = psum.tile([P, BANK], F32, name=f"h_acc{c}")
+            product(acc[:], w3_codes, w3_plane, c, 0, BANK)
+            nc.scalar.copy(h[:, BANK * c : BANK * (c + 1)], acc[:])
+        pick_e(1, 1, "w3")
+
+        gate = [keep.tile([P, T], F32, name=f"gate{d}") for d in range(2)]
+        for c in range(HALVES):
+            for d in range(2):
+                u = keep.tile([P, BANK], F32, name=f"u{d}{c}")
+                nc.vector.tensor_tensor(u[:], e_picked[d, c][:], y_acc[c][:], ALU.add)
+                nc.scalar.activation(gate[d][:, BANK * c : BANK * (c + 1)], u[:], ACT.Sigmoid)
+
+        for i, (lo, hi) in enumerate(OUT_CHUNKS):
+            passed = []
+            for d in range(2):
+                term = keep.tile([P, hi - lo], F32, name=f"term{d}{i}")
+                nc.vector.tensor_tensor(term[:], h[:].indirect(offsets(d, lo, hi)), gate[d][:, lo:hi], ALU.mult)
+                passed.append(term)
+            total = keep.tile([P, hi - lo], F32, name=f"total{i}")
+            nc.vector.tensor_tensor(total[:], passed[0][:], passed[1][:], ALU.add)
+            result = keep.tile([P, hi - lo], F32, name=f"result{i}")
+            nc.scalar.activation(result[:], total[:], ACT.Relu)
+            nc.scalar.dma_start(out[:, lo:hi], result[:])

@@ -22,6 +22,7 @@ PASSES = K // K_PASS
 BANK = 512
 HALVES = T // BANK
 LANES = 16
+X_PIECES = ((0, 0, 512), (1, 0, 512), (0, 512, 1024), (1, 512, 1024))
 OUT_CHUNKS = ((0, 512), (512, 768), (768, 896), (896, 1024))
 
 
@@ -47,6 +48,9 @@ def tile_picked_wgatedg_relu_l_kernel(
         x_plane = keep.tile([P, T], U8, align_bytes=64)
         nc.vector.memset(x_plane[:].bitcast(I32), 0)
 
+        warm_in = keep.tile([P, 1], F32)
+        warm_out = keep.tile([P, 1], F32)
+
         w2_raw = [keep.tile([P, K_PASS], F32, name=f"w2_raw{z}") for z in range(PASSES)]
         for z in range(PASSES):
             nc.sync.dma_start(w2_raw[z][:], weight_rows(w2)[:, z, :])
@@ -55,22 +59,20 @@ def tile_picked_wgatedg_relu_l_kernel(
                 x_plane[32 * q : 32 * q + 4 * PASSES, :].bitcast(I32),
                 x_scales[:, 4 * q : 4 * q + 4, :].bitcast(I32),
             )
+        nc.vector.memset(warm_in[:], 0.0)
+        nc.scalar.activation(warm_out[:], warm_in[:], ACT.Sigmoid)
 
-        x_codes = {}
-        for c in range(HALVES):
-            for z in range(PASSES):
-                x_codes[z, c] = keep.tile([P, BANK], U32, name=f"x_codes{z}{c}", align_bytes=64)
-                words = x_words[z].rearrange("p n t -> p (n t)")
-                nc.sync.dma_start(
-                    x_codes[z, c][:].bitcast(I32),
-                    words[:, PACK * BANK * c : PACK * BANK * (c + 1)].bitcast(I32),
-                )
-        nc.sync.dma_start(lists[0][:], pos1)
-        w1_raw = keep.tile([P, PASSES, K_PASS], F32)
-        nc.sync.dma_start(w1_raw[:], weight_rows(w1))
-        nc.sync.dma_start(lists[1][:], pos2)
-        w3_raw = keep.tile([P, PASSES, K_PASS], F32)
-        nc.sync.dma_start(w3_raw[:], weight_rows(w3))
+        x_codes = [keep.tile([P, T], U32, name=f"x_codes{z}", align_bytes=64) for z in range(PASSES)]
+        for z, lo, hi in X_PIECES:
+            words = x_words[z].rearrange("p n t -> p (n t)")
+            nc.sync.dma_start(x_codes[z][:, lo:hi].bitcast(I32), words[:, PACK * lo : PACK * hi].bitcast(I32))
+        w1_raw = [keep.tile([P, K_PASS], F32, name=f"w1_raw{z}") for z in range(PASSES)]
+        for z, pos in enumerate((pos1, pos2)):
+            nc.sync.dma_start(w1_raw[z][:], weight_rows(w1)[:, z, :])
+            nc.sync.dma_start(lists[z][:], pos)
+        w3_both = keep.tile([P, PASSES, K_PASS], F32, tag="w3_raw")
+        nc.sync.dma_start(w3_both[:], weight_rows(w3))
+        w3_raw = [w3_both[:, z, :] for z in range(PASSES)]
 
         def product(acc, codes, plane, c, lo, hi):
             for z in range(PASSES):
@@ -78,7 +80,7 @@ def tile_picked_wgatedg_relu_l_kernel(
                     acc,
                     lhsT=codes[z].bitcast(FP8X4),
                     lhsT_scale=plane[z],
-                    rhs=x_codes[z, c][:, lo:hi].bitcast(FP8X4),
+                    rhs=x_codes[z][:, BANK * c + lo : BANK * c + hi].bitcast(FP8X4),
                     rhs_scale=x_plane[4 * z : P, BANK * c + lo : BANK * c + hi],
                     start=(z == 0),
                     stop=(z == PASSES - 1),
@@ -108,7 +110,7 @@ def tile_picked_wgatedg_relu_l_kernel(
             codes = keep.tile([P, PASSES * M], U32, name=tag + "_codes", align_bytes=64)
             plane = keep.tile([P, PASSES * M], U8, name=tag + "_plane", align_bytes=64)
             for z in range(PASSES):
-                interleave(nc.scalar.copy, grouped[:, K_PASS * z : K_PASS * (z + 1)], raw[:, z, :])
+                interleave(nc.scalar.copy, grouped[:, K_PASS * z : K_PASS * (z + 1)], raw[z][:])
             nc.vector.quantize_mx(codes[:].bitcast(FP8X4), plane[:], grouped[:])
             return (
                 [codes[:, M * z : M * (z + 1)] for z in range(PASSES)],
@@ -122,17 +124,20 @@ def tile_picked_wgatedg_relu_l_kernel(
             nc.vector.tensor_copy(e_picked[d, c][:], e[:].indirect(offsets(d, BANK * c, BANK * (c + 1))))
 
         pick_e(0, 0, "pick00")
-        pick_e(1, 0, "pick10")
         w1_codes, w1_plane = quantized(w1_raw, "w1")
         y_acc = []
         for c in range(HALVES):
             acc = psum.tile([P, BANK], F32, name=f"y_acc{c}")
             product(acc[:], w1_codes, w1_plane, c, 0, BANK)
             y_acc.append(acc)
-        pick_e(0, 1, "w1")
+        middle = keep.tile([P, 2, BANK], F32, tag="w1", align_bytes=64)
+        for i, (d, c) in enumerate(((1, 0), (0, 1))):
+            e_picked[d, c] = middle[:, i, :]
+            nc.vector.tensor_copy(middle[:, i, :], e[:].indirect(offsets(d, BANK * c, BANK * (c + 1))))
         w3_codes, w3_plane = quantized(w3_raw, "w3")
+        y_first = keep.tile([P, BANK], F32, tag="w3_raw")
+        nc.scalar.copy(y_first[:], y_acc[0][:])
         h = keep.tile([P, T], F32)
-        h_acc = []
         for c in range(HALVES):
             acc = psum.tile([P, BANK], F32, name=f"h_acc{c}")
             product(acc[:], w3_codes, w3_plane, c, 0, BANK)
@@ -140,11 +145,14 @@ def tile_picked_wgatedg_relu_l_kernel(
         pick_e(1, 1, "w3")
 
         gate = [keep.tile([P, T], F32, name=f"gate{d}") for d in range(2)]
-        for c in range(HALVES):
-            for d in range(2):
-                u = keep.tile([P, BANK], F32, name=f"u{d}{c}")
-                nc.vector.tensor_tensor(u[:], e_picked[d, c][:], y_acc[c][:], ALU.add)
-                nc.scalar.activation(gate[d][:, BANK * c : BANK * (c + 1)], u[:], ACT.Sigmoid)
+        for d in range(2):
+            u = keep.tile([P, BANK], F32, name=f"u{d}0")
+            nc.gpsimd.tensor_tensor(u[:], e_picked[d, 0][:], y_first[:], ALU.add)
+            nc.scalar.activation(gate[d][:, 0:BANK], u[:], ACT.Sigmoid)
+        for d, tag in ((0, "pick00"), (1, "w1")):
+            u = keep.tile([P, BANK], F32, name=f"u{d}1", tag=tag, align_bytes=64)
+            nc.vector.tensor_tensor(u[:], e_picked[d, 1][:], y_acc[1][:], ALU.add)
+            nc.scalar.activation(gate[d][:, BANK:T], u[:], ACT.Sigmoid)
 
         for i, (lo, hi) in enumerate(OUT_CHUNKS):
             passed = []

@@ -1,6 +1,7 @@
 from contextlib import ExitStack
 
 import concourse.mybir as mybir
+from concourse.masks import make_identity
 
 K, T, M = 1024, 1024, 128
 FLOPS = 3 * 2 * K * T * M
@@ -22,8 +23,8 @@ PASSES = K // K_PASS
 BANK = 512
 HALVES = T // BANK
 LANES = 16
-X_PIECES = ((0, 0, 512), (1, 0, 512), (0, 512, 1024), (1, 512, 1024))
-OUT_CHUNKS = ((0, 512), (512, 768), (768, 896), (896, 1024))
+X_PIECES = ((0, 0, 512), (1, 0, 512), (0, 512, 1024), (1, 512, 768), (1, 768, 1024))
+OUT_CHUNKS = ((0, 256), (256, 512), (512, 768), (768, 896), (896, 1024))
 
 
 def tile_picked_wgatedg_relu_l_kernel(
@@ -51,28 +52,37 @@ def tile_picked_wgatedg_relu_l_kernel(
         warm_in = keep.tile([P, 1], F32)
         warm_out = keep.tile([P, 1], F32)
 
+        ident = keep.tile([P, P], F32)
+        make_identity(nc, ident[:])
+
+        nc.sync.dma_start(lists[0][:], pos1)
         w2_raw = [keep.tile([P, K_PASS], F32, name=f"w2_raw{z}") for z in range(PASSES)]
         for z in range(PASSES):
             nc.sync.dma_start(w2_raw[z][:], weight_rows(w2)[:, z, :])
+        x_codes = [keep.tile([P, T], U32, name=f"x_codes{z}", align_bytes=64) for z in range(PASSES)]
+
+        def load_x(z, lo, hi):
+            words = x_words[z].rearrange("p n t -> p (n t)")
+            nc.sync.dma_start(x_codes[z][:, lo:hi].bitcast(I32), words[:, PACK * lo : PACK * hi].bitcast(I32))
+
+        load_x(*X_PIECES[0])
         for q in range(4):
-            nc.scalar.dma_start(
+            nc.sync.dma_start(
                 x_plane[32 * q : 32 * q + 4 * PASSES, :].bitcast(I32),
                 x_scales[:, 4 * q : 4 * q + 4, :].bitcast(I32),
             )
+        for piece in X_PIECES[1:]:
+            load_x(*piece)
+        nc.sync.dma_start(lists[1][:], pos2)
+        w1_raw = [keep.tile([P, K_PASS], F32, name=f"w1_raw{z}") for z in range(PASSES)]
+        for z in range(PASSES):
+            nc.sync.dma_start(w1_raw[z][:], weight_rows(w1)[:, z, :])
+        w3_both = keep.tile([P, PASSES, K_PASS], F32, tag="w3_raw")
+        for z in range(PASSES):
+            nc.sync.dma_start(w3_both[:, z, :], weight_rows(w3)[:, z, :])
+        w3_raw = [w3_both[:, z, :] for z in range(PASSES)]
         nc.vector.memset(warm_in[:], 0.0)
         nc.scalar.activation(warm_out[:], warm_in[:], ACT.Sigmoid)
-
-        x_codes = [keep.tile([P, T], U32, name=f"x_codes{z}", align_bytes=64) for z in range(PASSES)]
-        for z, lo, hi in X_PIECES:
-            words = x_words[z].rearrange("p n t -> p (n t)")
-            nc.sync.dma_start(x_codes[z][:, lo:hi].bitcast(I32), words[:, PACK * lo : PACK * hi].bitcast(I32))
-        w1_raw = [keep.tile([P, K_PASS], F32, name=f"w1_raw{z}") for z in range(PASSES)]
-        for z, pos in enumerate((pos1, pos2)):
-            nc.sync.dma_start(w1_raw[z][:], weight_rows(w1)[:, z, :])
-            nc.sync.dma_start(lists[z][:], pos)
-        w3_both = keep.tile([P, PASSES, K_PASS], F32, tag="w3_raw")
-        nc.sync.dma_start(w3_both[:], weight_rows(w3))
-        w3_raw = [w3_both[:, z, :] for z in range(PASSES)]
 
         def product(acc, codes, plane, c, lo, hi):
             for z in range(PASSES):
@@ -98,7 +108,7 @@ def tile_picked_wgatedg_relu_l_kernel(
         e = keep.tile([P, T], F32)
         e_pieces = ((0, 0, 512, nc.scalar.copy), (1, 0, 256, nc.scalar.copy), (1, 256, 512, nc.vector.tensor_copy))
         for i, (c, lo, hi, copy) in enumerate(e_pieces):
-            acc = psum.tile([P, hi - lo], F32, name=f"e_acc{i}")
+            acc = psum.tile([P, hi - lo], F32, name=f"e_acc{i}", tag=f"e{i}")
             product(acc[:], w2_codes, w2_plane, c, lo, hi)
             copy(e[:, BANK * c + lo : BANK * c + hi], acc[:])
 
@@ -117,51 +127,81 @@ def tile_picked_wgatedg_relu_l_kernel(
                 [plane[:, M * z : M * (z + 1)] for z in range(PASSES)],
             )
 
-        e_picked = {}
+        def pick_e(picked, lo, hi):
+            for d in range(2):
+                nc.vector.tensor_copy(picked[:, d, :], e[:].indirect(offsets(d, lo, hi)))
 
-        def pick_e(d, c, tag):
-            e_picked[d, c] = keep.tile([P, BANK], F32, name=f"e_picked{d}{c}", tag=tag, align_bytes=64)
-            nc.vector.tensor_copy(e_picked[d, c][:], e[:].indirect(offsets(d, BANK * c, BANK * (c + 1))))
+        def both(row, width):
+            return row.unsqueeze(1).to_broadcast([P, 2, width])
 
-        pick_e(0, 0, "pick00")
+        first = keep.tile([P, 2, 256], F32)
+        pick_e(first, 0, 256)
         w1_codes, w1_plane = quantized(w1_raw, "w1")
         y_acc = []
-        for c in range(HALVES):
-            acc = psum.tile([P, BANK], F32, name=f"y_acc{c}")
-            product(acc[:], w1_codes, w1_plane, c, 0, BANK)
+        for c, lo, hi in ((0, 0, 256), (0, 256, 512), (1, 0, 512)):
+            acc = psum.tile([P, hi - lo], F32, name=f"y_acc{c}{lo}", tag=f"y{len(y_acc)}")
+            product(acc[:], w1_codes, w1_plane, c, lo, hi)
             y_acc.append(acc)
-        middle = keep.tile([P, 2, BANK], F32, tag="w1", align_bytes=64)
-        for i, (d, c) in enumerate(((1, 0), (0, 1))):
-            e_picked[d, c] = middle[:, i, :]
-            nc.vector.tensor_copy(middle[:, i, :], e[:].indirect(offsets(d, BANK * c, BANK * (c + 1))))
+        second = keep.tile([P, 2, 256], F32, tag="w1", align_bytes=64)
+        pick_e(second, 256, 512)
         w3_codes, w3_plane = quantized(w3_raw, "w3")
-        y_first = keep.tile([P, BANK], F32, tag="w3_raw")
-        nc.scalar.copy(y_first[:], y_acc[0][:])
+        y = keep.tile([P, T], F32, tag="w3_raw")
+        nc.scalar.copy(y[:, 0:256], y_acc[0][:])
+        nc.scalar.copy(y[:, 256:512], y_acc[1][:])
+        nc.scalar.copy(y[:, BANK:T], y_acc[2][:])
         h = keep.tile([P, T], F32)
         for c in range(HALVES):
-            acc = psum.tile([P, BANK], F32, name=f"h_acc{c}")
+            acc = psum.tile([P, BANK], F32, name=f"h_acc{c}", tag=f"h{c}")
             product(acc[:], w3_codes, w3_plane, c, 0, BANK)
             nc.scalar.copy(h[:, BANK * c : BANK * (c + 1)], acc[:])
-        pick_e(1, 1, "w3")
+        rest = keep.tile([P, 2, 2, 256], F32, tag="w3", align_bytes=64)
+        pick_e(rest[:, 0], 512, 768)
+        pick_e(rest[:, 1], 768, 1024)
 
-        gate = [keep.tile([P, T], F32, name=f"gate{d}") for d in range(2)]
-        for d in range(2):
-            u = keep.tile([P, BANK], F32, name=f"u{d}0")
-            nc.gpsimd.tensor_tensor(u[:], e_picked[d, 0][:], y_first[:], ALU.add)
-            nc.scalar.activation(gate[d][:, 0:BANK], u[:], ACT.Sigmoid)
-        for d, tag in ((0, "pick00"), (1, "w1")):
-            u = keep.tile([P, BANK], F32, name=f"u{d}1", tag=tag, align_bytes=64)
-            nc.vector.tensor_tensor(u[:], e_picked[d, 1][:], y_acc[1][:], ALU.add)
-            nc.scalar.activation(gate[d][:, BANK:T], u[:], ACT.Sigmoid)
+        def turned_sum(acc, blocks):
+            for b, (one, other) in enumerate(blocks):
+                nc.tensor.matmul(acc[:, P * b : P * (b + 1)], one, ident[:], start=True, stop=False, is_transpose=True)
+                nc.tensor.matmul(acc[:, P * b : P * (b + 1)], other, ident[:], start=False, stop=True, is_transpose=True)
+
+        def turn_back(acc, turned, count):
+            for b in range(count):
+                nc.tensor.transpose(acc[:, P * b : P * (b + 1)], turned[:, P * b : P * (b + 1)], ident[:])
+
+        gate = keep.tile([P, 2, T], F32)
+        for picked, lo, hi in ((first, 0, 256), (second, 256, 512)):
+            u = keep.tile([P, 2, hi - lo], F32, name=f"u{lo}")
+            nc.gpsimd.tensor_tensor(u[:], picked[:], both(y[:, lo:hi], hi - lo), ALU.add)
+            nc.scalar.activation(gate[:, :, lo:hi], u[:], ACT.Sigmoid)
+        turned = []
+        for j in range(2):
+            lo = BANK + 256 * j
+            acc = psum.tile([P, BANK], F32, name=f"turned_acc{j}", tag=f"h{j}")
+            turned_sum(acc, [(y[:, lo + P * b : lo + P * (b + 1)], rest[:, j, d, P * b : P * (b + 1)]) for d in range(2) for b in range(2)])
+            u = keep.tile([P, BANK], F32, name=f"turned{j}")
+            nc.scalar.copy(u[:], acc[:])
+            turned.append(u)
+        for j in range(2):
+            lo = BANK + 256 * j
+            acc = psum.tile([P, BANK], F32, name=f"back_acc{j}", tag=f"e{j}")
+            turn_back(acc, turned[j], 4)
+            nc.scalar.activation(gate[:, :, lo : lo + 256], acc[:].rearrange("p (d v) -> p d v", d=2), ACT.Sigmoid)
 
         for i, (lo, hi) in enumerate(OUT_CHUNKS):
-            passed = []
+            terms = keep.tile([P, 2, hi - lo], F32, name=f"terms{i}", tag="w1" if i == 0 else f"terms{i}", align_bytes=64)
             for d in range(2):
-                term = keep.tile([P, hi - lo], F32, name=f"term{d}{i}")
-                nc.vector.tensor_tensor(term[:], h[:].indirect(offsets(d, lo, hi)), gate[d][:, lo:hi], ALU.mult)
-                passed.append(term)
-            total = keep.tile([P, hi - lo], F32, name=f"total{i}")
-            nc.vector.tensor_tensor(total[:], passed[0][:], passed[1][:], ALU.add)
+                nc.vector.tensor_tensor(terms[:, d, :], h[:].indirect(offsets(d, lo, hi)), gate[:, d, lo:hi], ALU.mult)
             result = keep.tile([P, hi - lo], F32, name=f"result{i}")
-            nc.scalar.activation(result[:], total[:], ACT.Relu)
-            nc.scalar.dma_start(out[:, lo:hi], result[:])
+            if i < 2:
+                acc = psum.tile([P, 256], F32, name=f"sum_acc{i}", tag=f"y{i}")
+                turned_sum(acc, [(terms[:, 0, P * b : P * (b + 1)], terms[:, 1, P * b : P * (b + 1)]) for b in range(2)])
+                total = keep.tile([P, 256], F32, name=f"total{i}")
+                nc.scalar.activation(total[:], acc[:], ACT.Relu)
+                back = psum.tile([P, 256], F32, name=f"sum_back{i}", tag=("e2", "y2")[i])
+                turn_back(back, total, 2)
+                nc.scalar.copy(result[:], back[:])
+                nc.sync.dma_start(out[:, lo:hi], result[:])
+            else:
+                total = keep.tile([P, hi - lo], F32, name=f"total{i}")
+                nc.vector.tensor_tensor(total[:], terms[:, 0, :], terms[:, 1, :], ALU.add)
+                nc.scalar.activation(result[:], total[:], ACT.Relu)
+                nc.scalar.dma_start(out[:, lo:hi], result[:])

from contextlib import ExitStack

import concourse.mybir as mybir
from concourse.masks import make_identity

K, T, M = 1024, 1024, 128
FLOPS = 3 * 2 * K * T * M

F32 = mybir.dt.float32
BF16 = mybir.dt.bfloat16
I32 = mybir.dt.int32
U32 = mybir.dt.uint32
U16 = mybir.dt.uint16
U8 = mybir.dt.uint8
FP8X4 = mybir.dt.float8_e4m3fn_x4
ALU = mybir.AluOpType
ACT = mybir.ActivationFunctionType

P = 128
PACK = 4
K_PASS = P * PACK
PASSES = K // K_PASS
BANK = 512
HALVES = T // BANK
LANES = 16
X_PIECES = ((0, 0, 512), (1, 0, 512), (0, 512, 1024), (1, 512, 768), (1, 768, 1024))
OUT_CHUNKS = ((0, 256), (256, 512), (512, 768), (768, 896), (896, 1024))


def tile_picked_wgatedg_relu_l_kernel(
    tc, x_words, x_scales, w1, w2, w3, pos1, pos2, out
):
    nc = tc.nc

    def interleave(copy, grouped, raw):
        copy(
            grouped.rearrange("p (c i t) -> p c t i", i=4, t=PACK),
            raw.rearrange("p (t c i) -> p c t i", i=4, t=PACK),
        )

    def weight_rows(w):
        return w.rearrange("(z p t) m -> p z (t m)", z=PASSES, t=PACK)

    with ExitStack() as ctx:
        keep = ctx.enter_context(tc.tile_pool(name="keep", bufs=1))
        psum = ctx.enter_context(tc.psum_pool(name="psum", bufs=1))

        lists = [keep.tile([P, T // LANES], U16, name=f"list{d}") for d in range(2)]
        x_plane = keep.tile([P, T], U8, align_bytes=64)
        nc.vector.memset(x_plane[:].bitcast(I32), 0)

        warm_in = keep.tile([P, 1], F32)
        warm_out = keep.tile([P, 1], F32)

        ident = keep.tile([P, P], F32)
        make_identity(nc, ident[:])

        nc.sync.dma_start(lists[0][:], pos1)
        w2_raw = [keep.tile([P, K_PASS], F32, name=f"w2_raw{z}") for z in range(PASSES)]
        for z in range(PASSES):
            nc.sync.dma_start(w2_raw[z][:], weight_rows(w2)[:, z, :])
        x_codes = [keep.tile([P, T], U32, name=f"x_codes{z}", align_bytes=64) for z in range(PASSES)]

        def load_x(z, lo, hi):
            words = x_words[z].rearrange("p n t -> p (n t)")
            nc.sync.dma_start(x_codes[z][:, lo:hi].bitcast(I32), words[:, PACK * lo : PACK * hi].bitcast(I32))

        load_x(*X_PIECES[0])
        for q in range(4):
            nc.sync.dma_start(
                x_plane[32 * q : 32 * q + 4 * PASSES, :].bitcast(I32),
                x_scales[:, 4 * q : 4 * q + 4, :].bitcast(I32),
            )
        for piece in X_PIECES[1:]:
            load_x(*piece)
        nc.sync.dma_start(lists[1][:], pos2)
        w1_raw = [keep.tile([P, K_PASS], F32, name=f"w1_raw{z}") for z in range(PASSES)]
        for z in range(PASSES):
            nc.sync.dma_start(w1_raw[z][:], weight_rows(w1)[:, z, :])
        w3_both = keep.tile([P, PASSES, K_PASS], F32, tag="w3_raw")
        for z in range(PASSES):
            nc.sync.dma_start(w3_both[:, z, :], weight_rows(w3)[:, z, :])
        w3_raw = [w3_both[:, z, :] for z in range(PASSES)]
        nc.vector.memset(warm_in[:], 0.0)
        nc.scalar.activation(warm_out[:], warm_in[:], ACT.Sigmoid)

        def product(acc, codes, plane, c, lo, hi):
            for z in range(PASSES):
                nc.tensor.matmul_mx(
                    acc,
                    lhsT=codes[z].bitcast(FP8X4),
                    lhsT_scale=plane[z],
                    rhs=x_codes[z][:, BANK * c + lo : BANK * c + hi].bitcast(FP8X4),
                    rhs_scale=x_plane[4 * z : P, BANK * c + lo : BANK * c + hi],
                    start=(z == 0),
                    stop=(z == PASSES - 1),
                )

        w2_codes, w2_plane = [], []
        for z in range(PASSES):
            grouped = keep.tile([P, K_PASS], BF16, name=f"w2_grouped{z}", align_bytes=64)
            codes = keep.tile([P, M], U32, name=f"w2_codes{z}", align_bytes=64)
            plane = keep.tile([P, M], U8, name=f"w2_plane{z}", align_bytes=64)
            interleave(nc.vector.tensor_copy, grouped[:], w2_raw[z][:])
            nc.vector.quantize_mx(codes[:].bitcast(FP8X4), plane[:], grouped[:])
            w2_codes.append(codes[:])
            w2_plane.append(plane[:])
        e = keep.tile([P, T], F32)
        e_pieces = ((0, 0, 512, nc.scalar.copy), (1, 0, 256, nc.scalar.copy), (1, 256, 512, nc.vector.tensor_copy))
        for i, (c, lo, hi, copy) in enumerate(e_pieces):
            acc = psum.tile([P, hi - lo], F32, name=f"e_acc{i}", tag=f"e{i}")
            product(acc[:], w2_codes, w2_plane, c, lo, hi)
            copy(e[:, BANK * c + lo : BANK * c + hi], acc[:])

        def offsets(d, lo, hi):
            return lists[d][:, lo // LANES : hi // LANES]

        def quantized(raw, tag):
            grouped = keep.tile([P, K], BF16, name=tag + "_grouped", tag=tag, align_bytes=64)
            codes = keep.tile([P, PASSES * M], U32, name=tag + "_codes", align_bytes=64)
            plane = keep.tile([P, PASSES * M], U8, name=tag + "_plane", align_bytes=64)
            for z in range(PASSES):
                interleave(nc.scalar.copy, grouped[:, K_PASS * z : K_PASS * (z + 1)], raw[z][:])
            nc.vector.quantize_mx(codes[:].bitcast(FP8X4), plane[:], grouped[:])
            return (
                [codes[:, M * z : M * (z + 1)] for z in range(PASSES)],
                [plane[:, M * z : M * (z + 1)] for z in range(PASSES)],
            )

        def pick_e(picked, lo, hi):
            for d in range(2):
                nc.vector.tensor_copy(picked[:, d, :], e[:].indirect(offsets(d, lo, hi)))

        def both(row, width):
            return row.unsqueeze(1).to_broadcast([P, 2, width])

        first = keep.tile([P, 2, 256], F32)
        pick_e(first, 0, 256)
        w1_codes, w1_plane = quantized(w1_raw, "w1")
        y_acc = []
        for c, lo, hi in ((0, 0, 256), (0, 256, 512), (1, 0, 512)):
            acc = psum.tile([P, hi - lo], F32, name=f"y_acc{c}{lo}", tag=f"y{len(y_acc)}")
            product(acc[:], w1_codes, w1_plane, c, lo, hi)
            y_acc.append(acc)
        second = keep.tile([P, 2, 256], F32, tag="w1", align_bytes=64)
        pick_e(second, 256, 512)
        w3_codes, w3_plane = quantized(w3_raw, "w3")
        y = keep.tile([P, T], F32, tag="w3_raw")
        nc.scalar.copy(y[:, 0:256], y_acc[0][:])
        nc.scalar.copy(y[:, 256:512], y_acc[1][:])
        nc.scalar.copy(y[:, BANK:T], y_acc[2][:])
        h = keep.tile([P, T], F32)
        for c in range(HALVES):
            acc = psum.tile([P, BANK], F32, name=f"h_acc{c}", tag=f"h{c}")
            product(acc[:], w3_codes, w3_plane, c, 0, BANK)
            nc.scalar.copy(h[:, BANK * c : BANK * (c + 1)], acc[:])
        rest = keep.tile([P, 2, 2, 256], F32, tag="w3", align_bytes=64)
        pick_e(rest[:, 0], 512, 768)
        pick_e(rest[:, 1], 768, 1024)

        def turned_sum(acc, blocks):
            for b, (one, other) in enumerate(blocks):
                nc.tensor.matmul(acc[:, P * b : P * (b + 1)], one, ident[:], start=True, stop=False, is_transpose=True)
                nc.tensor.matmul(acc[:, P * b : P * (b + 1)], other, ident[:], start=False, stop=True, is_transpose=True)

        def turn_back(acc, turned, count):
            for b in range(count):
                nc.tensor.transpose(acc[:, P * b : P * (b + 1)], turned[:, P * b : P * (b + 1)], ident[:])

        gate = keep.tile([P, 2, T], F32)
        for picked, lo, hi in ((first, 0, 256), (second, 256, 512)):
            u = keep.tile([P, 2, hi - lo], F32, name=f"u{lo}")
            nc.gpsimd.tensor_tensor(u[:], picked[:], both(y[:, lo:hi], hi - lo), ALU.add)
            nc.scalar.activation(gate[:, :, lo:hi], u[:], ACT.Sigmoid)
        turned = []
        for j in range(2):
            lo = BANK + 256 * j
            acc = psum.tile([P, BANK], F32, name=f"turned_acc{j}", tag=f"h{j}")
            turned_sum(acc, [(y[:, lo + P * b : lo + P * (b + 1)], rest[:, j, d, P * b : P * (b + 1)]) for d in range(2) for b in range(2)])
            u = keep.tile([P, BANK], F32, name=f"turned{j}")
            nc.scalar.copy(u[:], acc[:])
            turned.append(u)
        for j in range(2):
            lo = BANK + 256 * j
            acc = psum.tile([P, BANK], F32, name=f"back_acc{j}", tag=f"e{j}")
            turn_back(acc, turned[j], 4)
            nc.scalar.activation(gate[:, :, lo : lo + 256], acc[:].rearrange("p (d v) -> p d v", d=2), ACT.Sigmoid)

        for i, (lo, hi) in enumerate(OUT_CHUNKS):
            terms = keep.tile([P, 2, hi - lo], F32, name=f"terms{i}", tag="w1" if i == 0 else f"terms{i}", align_bytes=64)
            for d in range(2):
                nc.vector.tensor_tensor(terms[:, d, :], h[:].indirect(offsets(d, lo, hi)), gate[:, d, lo:hi], ALU.mult)
            result = keep.tile([P, hi - lo], F32, name=f"result{i}")
            if i < 2:
                acc = psum.tile([P, 256], F32, name=f"sum_acc{i}", tag=f"y{i}")
                turned_sum(acc, [(terms[:, 0, P * b : P * (b + 1)], terms[:, 1, P * b : P * (b + 1)]) for b in range(2)])
                total = keep.tile([P, 256], F32, name=f"total{i}")
                nc.scalar.activation(total[:], acc[:], ACT.Relu)
                back = psum.tile([P, 256], F32, name=f"sum_back{i}", tag=("e2", "y2")[i])
                turn_back(back, total, 2)
                nc.scalar.copy(result[:], back[:])
                nc.sync.dma_start(out[:, lo:hi], result[:])
            else:
                total = keep.tile([P, hi - lo], F32, name=f"total{i}")
                nc.vector.tensor_tensor(total[:], terms[:, 0, :], terms[:, 1, :], ALU.add)
                nc.scalar.activation(result[:], total[:], ACT.Relu)
                nc.scalar.dma_start(out[:, lo:hi], result[:])
